import numpy as np
import ml_dtypes


def mxq(x, axis, fmt="e4m3"):
    dtype, down = {"e4m3": (ml_dtypes.float8_e4m3fn, 7), "e5m2": (ml_dtypes.float8_e5m2, 14)}[fmt]
    v = np.moveaxis(np.asarray(x, np.float32).astype(ml_dtypes.bfloat16).astype(np.float64), axis, -1)
    blocks = v.reshape(v.shape[:-1] + (-1, 32))
    amax = np.abs(blocks).max(-1, keepdims=True)
    byte = np.maximum(np.where(amax > 0, np.frexp(amax)[1] - 1 + 127, 0) - down, 1)
    scale = np.exp2(byte - 127.0)
    codes = (blocks / scale).astype(np.float32).astype(dtype).astype(np.float64)
    return np.moveaxis((codes * scale).reshape(v.shape), -1, axis)


WIDE = False


def mx_kscale(k):
    if not WIDE:
        return np.ones(k)
    levels = np.array([10, -10, 5, -5, 0])
    if k % 512:
        return np.exp2(np.random.permutation(np.resize(levels, k // 32))).repeat(32)
    a = np.empty((k // 512, 16))
    for p in range(k // 512):
        a[p, :8] = np.random.permutation(np.resize(levels, 8))
        for g in range(8):
            far = levels[np.abs(levels - a[p, g]) >= 10]
            a[p, g + 8] = far[np.random.randint(len(far))]
    return np.exp2(a.ravel()).repeat(32)


def f64(x):
    return np.asarray(x).astype(np.float64)


def striped(idx):
    return np.tile(idx.reshape(-1, 16).T, (8, 1)).astype(np.uint16)


def unstriped(offs):
    return offs[:16].T.reshape(-1).astype(np.int64)


E2M1 = np.array([0.0, 0.5, 1.0, 1.5, 2.0, 3.0, 4.0, 6.0, -0.0, -0.5, -1.0, -1.5, -2.0, -3.0, -4.0, -6.0])


def pack_weight(w, fmt):
    k, n = w.shape
    w = f64(np.asarray(w, np.float32).astype(ml_dtypes.bfloat16)).reshape(k // 32, 32, n)
    amax = np.abs(w).max(1)
    if fmt == "e4m3":
        byte = np.frexp(amax)[1] - 1 + 127 - 7
    else:
        mant, ex = np.frexp(amax / 6.0)
        byte = np.where(mant > 0.5, ex, ex - 1) + 127
    byte = np.clip(np.where(amax > 0, byte, 1), 1, 254)
    scaled = (w * np.exp2(127.0 - byte)[:, None, :]).reshape(k, n).astype(np.float32)
    by_word = np.ascontiguousarray(scaled.reshape(k // 512, 128, 4, n).transpose(0, 1, 3, 2))
    if fmt == "e4m3":
        words = by_word.astype(ml_dtypes.float8_e4m3fn).view(np.uint8)
    else:
        c = by_word.astype(ml_dtypes.float4_e2m1fn).view(np.uint8) & 0xF
        words = (c[..., 0::2] | (c[..., 1::2] << 4)).reshape(k // 512, 128, 2 * n)
    return np.ascontiguousarray(words), np.ascontiguousarray(byte.astype(np.uint8).reshape(k // 512, 16, n))


def unpack_weight(words, scales, fmt):
    g, _, n = scales.shape
    words = np.ascontiguousarray(words).reshape(g, 128, n, -1)
    if fmt == "e4m3":
        vals = words.view(ml_dtypes.float8_e4m3fn).astype(np.float64)
    else:
        nib = np.empty((g, 128, n, 4), np.uint8)
        nib[..., 0::2] = words & 0xF
        nib[..., 1::2] = words >> 4
        vals = E2M1[nib]
    vals = vals * np.repeat(np.exp2(scales.astype(np.float64) - 127.0), 8, axis=1)[..., None]
    return vals.transpose(0, 1, 3, 2).reshape(g * 512, n)


def gelu(v):
    return 0.5 * v * (1.0 + np.tanh(np.sqrt(2.0 / np.pi) * (v + 0.044715 * v**3)))


def bf(x):
    return np.asarray(x, np.float32).astype(ml_dtypes.bfloat16)


def planes(Y):
    n, m = Y.shape
    b = f64(bf(Y)).reshape(n // 32, 32, m)
    amax = np.abs(b).max(1)
    byte = np.clip(np.where(amax > 0, np.frexp(amax)[1] - 1 + 127 - 7, 1), 1, 254)
    codes = (b * np.exp2(127.0 - byte)[:, None, :]).reshape(n, m).astype(np.float32).astype(ml_dtypes.float8_e4m3fn).view(np.uint8)
    words = codes.reshape(n // 512, 128, 4, m).transpose(0, 1, 3, 2)
    return np.ascontiguousarray(words), np.ascontiguousarray(byte.astype(np.uint8).reshape(n // 512, 16, m))


K, T, S, H, T2, P, N = 1536, 2048, 1024, 1024, 2048, 512, 384

def setup_inputs():
    n = np.random.standard_normal
    s = mx_kscale(K)[:, None]
    u = mx_kscale(H)[:, None]
    d = {}
    d["tab_words"], d["tab_scales"] = pack_weight(n((K, T)) * s, "e4m3")
    d["offs"] = striped(np.random.permutation(T)[:S])
    d["offs2"] = striped(np.random.permutation(T2)[:S])
    d["offs3"] = striped(np.random.permutation(T2)[:P])
    d["w1"] = (1.5 * n((K, H)) / K ** 0.5 / s).astype(np.float32)
    d["gain"] = (np.exp(0.3 * n(H)) * u[:, 0]).astype(np.float32)
    d["wgs"] = np.exp(0.3 * n((128, S))).astype(np.float32)
    d["page0"] = (n((H, T2)) * u).astype(np.float32)
    d["bx"] = (0.6 * n(H) * u[:, 0]).astype(np.float32)
    d["w4_words"], d["w4_scales"] = pack_weight(n((H, N)) / H ** 0.5 / u, "e2m1")
    d["w5"] = (n((H, N)) / H ** 0.5 / u).astype(np.float32)
    return d

def reference(tab_words, tab_scales, offs, offs2, offs3, w1, gain, wgs, page0, bx, w4_words, w4_scales, w5):
    v = unpack_weight(tab_words, tab_scales, "e4m3")[:, unstriped(offs)]
    a = mxq(f64(w1), 0, "e4m3").T @ v
    h = f64(gain)[:, None] * (a / (1.0 + np.exp(-a)))
    page = f64(page0).copy()
    page[:, unstriped(offs2)] = np.tile(f64(wgs), (H // 128, 1)) * h
    x = page[:, unstriped(offs3)] + f64(bx)[:, None]
    xq = mxq(x, 0, "e4m3")
    y1 = unpack_weight(w4_words, w4_scales, "e2m1").T @ xq
    y2 = mxq(f64(w5), 0, "e4m3").T @ xq
    y = y1 * np.cos(2.0 * np.tanh(y2))
    words, scales = planes(page)
    return y, page, words, scales

@@ -1,0 +1,367 @@
+import math
+from contextlib import ExitStack
+
+import concourse.mybir as mybir
+from concourse.masks import make_identity
+
+K, T, S, H, T2, M, N = 1536, 2048, 1024, 1024, 2048, 512, 384
+FLOPS = 2 * K * H * S + 2 * 2 * H * N * M
+
+F32 = mybir.dt.float32
+BF16 = mybir.dt.bfloat16
+I32 = mybir.dt.int32
+U32 = mybir.dt.uint32
+U16 = mybir.dt.uint16
+U8 = mybir.dt.uint8
+FP8X4 = mybir.dt.float8_e4m3fn_x4
+FP4X4 = mybir.dt.float4_e2m1fn_x4
+ACT = mybir.ActivationFunctionType
+ALU = mybir.AluOpType
+
+P = 128
+PACK = 4
+KP = P * PACK
+BANK = 512
+PASSES_K = K // KP
+GROUPS = H // KP
+CHUNKS = T2 // BANK
+PAGE_BUFS = 6
+KB = 1024
+REGION_A, REGION_B, REGION_C, REGION_D, REGION_E = 0, 32 * KB, 56 * KB, 80 * KB, 104 * KB
+RAW_OFFSETS = [[REGION_B + 8 * KB * a for a in range(PASSES_K)], [REGION_C + 8 * KB * a for a in range(PASSES_K)]]
+SLOT = [REGION_D + 4 * KB * k for k in range(6)]
+GOT_S, GOT_W = REGION_E, [REGION_E + 9 * KB, REGION_E + KB, REGION_E + 5 * KB]
+GROUPED_OFFSETS = [[GOT_S, SLOT[5], GOT_W[2]], [SLOT[0], SLOT[1], SLOT[2]]]
+ACT_OFFSETS = [SLOT[1], SLOT[3], SLOT[5], SLOT[3], SLOT[5], SLOT[3], SLOT[5], SLOT[3]]
+FACTOR_OFFSETS = [SLOT[0], SLOT[2], SLOT[4], RAW_OFFSETS[1][2], SLOT[4], RAW_OFFSETS[0][1], REGION_A, REGION_A + 16 * KB]
+WOVEN_OFFSETS = [[REGION_C + 4 * KB * c for c in range(CHUNKS)], [REGION_C + 4 * KB * ((c + 4) % 6) for c in range(CHUNKS)]]
+HALF = T2 // 2
+
+
+def tile_list_cue_brightness_desk_kernel(
+    tc, tab_words, tab_scales, offs, offs2, offs3, w1, gain, wgs, page0, bx, w4_words, w4_scales, w5,
+    out_0, out_1, out_2, out_3,
+):
+    nc = tc.nc
+    with ExitStack() as ctx:
+        lists = ctx.enter_context(tc.tile_pool(name="lists", bufs=1))
+        keep = ctx.enter_context(tc.tile_pool(name="keep", bufs=1))
+        shared = ctx.enter_context(tc.tile_pool(name="shared", bufs=1))
+        ring = ctx.enter_context(tc.tile_pool(name="ring", bufs=2))
+        psum = ctx.enter_context(tc.psum_pool(name="psum", bufs=4))
+
+        page_in = page0.rearrange("(b p t) m -> b t p m", b=GROUPS, t=PACK)
+        page_out = out_1.rearrange("(b p t) m -> b t p m", b=GROUPS, t=PACK)
+
+        idx1 = lists.tile([P, S // 16], U16, name="idx1")
+        idx2 = lists.tile([P, S // 16], U16, name="idx2")
+        idx3 = lists.tile([P, M // 16], U16, name="idx3")
+
+        ident = keep.tile([P, P], F32, name="ident")
+        make_identity(nc, ident[:])
+        tab_s = keep.tile([P, T], U8, name="tab_s", align_bytes=64)
+        nc.vector.memset(tab_s[:].bitcast(I32), 0)
+        w4_s = keep.tile([P, GROUPS * N], U8, name="w4_s", align_bytes=64)
+        nc.vector.memset(w4_s[:].bitcast(I32), 0)
+        half_pi = keep.tile([P, 1], F32, name="half_pi")
+        one = keep.tile([P, 1], F32, name="one")
+        nc.vector.memset(one[:], 1.0)
+        nc.vector.tensor_scalar(half_pi[:], one[:], math.pi / 2, None, ALU.mult)
+
+        for q in range(4):
+            nc.scalar.dma_start(
+                out=tab_s[32 * q : 32 * q + 4 * PASSES_K, :].bitcast(I32),
+                in_=tab_scales[:, 4 * q : 4 * q + 4, :].bitcast(I32),
+            )
+        gain_c = keep.tile([P, GROUPS, PACK], F32, name="gain_c")
+        bx_c = keep.tile([P, GROUPS, PACK], F32, name="bx_c")
+
+        tab_w = [shared.tile([P, T], I32, name=f"tab_w{a}", offset=a * T * 4) for a in range(PASSES_K)]
+        got_w = [shared.tile([P, S], U32, name=f"got_w{a}", align_bytes=64, offset=GOT_W[a]) for a in range(PASSES_K)]
+        got_s = shared.tile([P, S], U8, name="got_s", align_bytes=64, offset=GOT_S)
+        w1_c = keep.tile([P, GROUPS * PASSES_K, KP], U32, name="w1_c", align_bytes=64)
+        w1_s = keep.tile([P, GROUPS * PASSES_K, KP], U8, name="w1_s", align_bytes=64)
+        wgs_t = keep.tile([P, S // P * PACK * P], F32, name="wgs_t")
+
+        def load_table(a):
+            nc.sync.dma_start(out=tab_w[a][:], in_=tab_words[a].rearrange("p t i -> p (t i)").bitcast(I32))
+
+        def gather_table(a, half):
+            cols = slice(half * BANK, (half + 1) * BANK)
+            nc.vector.tensor_copy(got_w[a][:, cols], tab_w[a][:].bitcast(U32).indirect(idx1[:, half * 32 : (half + 1) * 32]))
+
+        def load_w1(b, a):
+            raw = shared.tile([P, PACK, KP], F32, name=f"raw{b}{a}", offset=RAW_OFFSETS[b][a])
+            rows = w1[a * KP : (a + 1) * KP, b * KP : (b + 1) * KP]
+            nc.sync.dma_start(out=raw[:], in_=rows.rearrange("(p j) c -> p j c", j=PACK))
+            return raw
+
+        def prepare_w1(b, a, raw):
+            grouped = shared.tile(
+                [P, PACK * KP], BF16, name=f"grouped{b}{a}", align_bytes=64, offset=GROUPED_OFFSETS[b][a]
+            )
+            nc.scalar.copy(
+                out=grouped[:].rearrange("p (t m j) -> p m j t", t=PACK, j=PACK),
+                in_=raw[:].rearrange("p j (m t) -> p m j t", t=PACK),
+            )
+            g = b * PASSES_K + a
+            nc.vector.quantize_mx(out=w1_c[:, g, :].bitcast(FP8X4), scales=w1_s[:, g, :], in_=grouped[:])
+
+        def load_page(i):
+            page = ring.tile([P, T2], F32, name="page", bufs=PAGE_BUFS)
+            nc.sync.dma_start(out=page[:], in_=page_in[i // PACK, i % PACK])
+            return page
+
+        nc.sync.dma_start(idx1[:], offs)
+        wgs_sb = shared.tile([P, S], F32, name="wgs_sb", offset=SLOT[4])
+        nc.sync.dma_start(out=wgs_sb[:], in_=wgs)
+        load_table(0)
+        nc.sync.dma_start(out=gain_c[:], in_=gain.rearrange("(b p t) -> p b t", b=GROUPS, t=PACK))
+        raw00 = load_w1(0, 0)
+        load_table(1)
+        raw01 = load_w1(0, 1)
+        raw02 = load_w1(0, 2)
+        load_table(2)
+        nc.sync.dma_start(idx2[:], offs2)
+        pages = [load_page(0)]
+        nc.sync.dma_start(idx3[:], offs3)
+        nc.sync.dma_start(out=bx_c[:], in_=bx.rearrange("(b p t) -> p b t", b=GROUPS, t=PACK))
+
+        dealt = wgs_t[:].rearrange("j (jb t r q) -> j jb t r q", t=PACK, r=4, q=32)
+        for half in range(2):
+            bank = psum.tile([P, BANK], F32, name="work")
+            for jj in range(4):
+                jb = 4 * half + jj
+                nc.tensor.transpose(bank[:, jj * P : (jj + 1) * P], wgs_sb[:, jb * P : (jb + 1) * P], ident[:])
+            nc.scalar.copy(
+                out=dealt[:, 4 * half : 4 * half + 4, :, 0, :],
+                in_=bank[:].rearrange("j (jb q t) -> j jb t q", q=32, t=PACK),
+            )
+        gather_table(0, 0)
+        gather_table(0, 1)
+        for r in range(1, 4):
+            nc.vector.tensor_copy(out=dealt[:, :, :, r, :], in_=dealt[:, :, :, 0, :])
+        prepare_w1(0, 0, raw00)
+        gather_table(1, 0)
+        gather_table(1, 1)
+        nc.vector.tensor_copy(got_s[:], tab_s[:].indirect(idx1[:]))
+        prepare_w1(0, 1, raw01)
+        prepare_w1(0, 2, raw02)
+        gather_table(2, 0)
+        gather_table(2, 1)
+
+        def features(i):
+            b, t = divmod(i, PACK)
+            factor = shared.tile([P, S], F32, name=f"factor{i}", offset=FACTOR_OFFSETS[i])
+            act = shared.tile([P, S], F32, name=f"act{i}", offset=ACT_OFFSETS[i])
+            for half in range(2):
+                cols = slice(half * BANK, (half + 1) * BANK)
+                bank = psum.tile([P, BANK], F32, name="work")
+                for jj in range(4):
+                    start = ((4 * half + jj) * PACK + t) * P
+                    nc.tensor.transpose(bank[:, jj * P : (jj + 1) * P], wgs_t[:, start : start + P], ident[:])
+                nc.scalar.activation(out=factor[:, cols], in_=bank[:], func=ACT.Copy, scale=gain_c[:, b, t : t + 1])
+            for half in range(2):
+                cols = slice(half * BANK, (half + 1) * BANK)
+                acc = psum.tile([P, BANK], F32, name="work")
+                for a in range(PASSES_K):
+                    g = b * PASSES_K + a
+                    nc.tensor.matmul_mx(
+                        out=acc[:],
+                        lhsT=w1_c[:, g, t * P : (t + 1) * P].bitcast(FP8X4),
+                        lhsT_scale=w1_s[:, g, t * P : (t + 1) * P],
+                        rhs=got_w[a][:, cols].bitcast(FP8X4),
+                        rhs_scale=got_s[4 * a : P, cols],
+                        start=(a == 0),
+                        stop=(a == PASSES_K - 1),
+                    )
+                nc.scalar.activation(out=act[:, cols], in_=acc[:], func=ACT.Silu)
+            return act, factor
+
+        def scatter(i, act, factor):
+            pieces = 2 if i == 0 else 1
+            n = S // pieces
+            for k in range(pieces):
+                nc.vector.tensor_tensor(
+                    pages[i][:].indirect(idx2[:, k * n // 16 : (k + 1) * n // 16]),
+                    act[:, k * n : (k + 1) * n],
+                    factor[:, k * n : (k + 1) * n],
+                    ALU.mult,
+                )
+
+        rows0 = [shared.tile([P, PACK, HALF], F32, name=f"rows0{h}", offset=REGION_A + 16 * KB * h) for h in range(2)]
+        rows1_lo = [shared.tile([P, 2, HALF], F32, name=f"rows1_lo{h}", offset=REGION_B + 16 * KB * h) for h in range(2)]
+        rows1_hi = shared.tile([P, 2, T2], F32, name="rows1_hi", offset=REGION_A)
+        x_rows = [shared.tile([P, PACK, M], BF16, name=f"x_rows{b}", offset=REGION_B) for b in range(GROUPS)]
+        x_c = keep.tile([P, GROUPS, M], U32, name="x_c", align_bytes=64)
+        x_s = keep.tile([P, GROUPS, M], U8, name="x_s", align_bytes=64)
+        plane_s = [keep.tile([P, T2], U8, name=f"plane_s{b}", align_bytes=64) for b in range(GROUPS)]
+        words_out = [out_2[b].rearrange("p m i -> p (m i)").bitcast(I32) for b in range(GROUPS)]
+
+        picked = [ring.tile([P, PACK, M], F32, name="picked", bufs=1) for b in range(GROUPS)]
+
+        def fetch(i):
+            b, t = divmod(i, PACK)
+            nc.vector.tensor_copy(picked[b][:, t, :], pages[i][:].indirect(idx3[:]))
+
+        def hand_out(i):
+            b, t = divmod(i, PACK)
+            if i < PACK + 2:
+                for h in range(2):
+                    rows = rows0[h] if b == 0 else rows1_lo[h]
+                    nc.sync.dma_start(out=rows[:, t, :], in_=pages[i][:, h * HALF : (h + 1) * HALF])
+            elif i == PACK + 2:
+                nc.sync.dma_start(out=rows1_hi[:, 0, :], in_=pages[i][:])
+            nc.sync.dma_start(out=page_out[b, t], in_=pages[i][:])
+
+        def add_bias(b, t, out):
+            nc.scalar.activation(out=out, in_=picked[b][:, t, :], func=ACT.Identity, bias=bx_c[:, b, t : t + 1])
+
+        def weave(copy, woven, rows, first, count):
+            copy(
+                out=woven[:].rearrange("p (c i t) -> p c t i", i=4, t=PACK)[:, :, first : first + count, :],
+                in_=rows.rearrange("p t (c i) -> p c t i", i=4),
+            )
+
+        def new_woven(b, c):
+            return shared.tile(
+                [P, PACK * BANK], BF16, name=f"woven{b}{c}", align_bytes=64, offset=WOVEN_OFFSETS[b][c]
+            )
+
+        def quantize_planes(b, c, woven):
+            cols = slice(c * BANK, (c + 1) * BANK)
+            words = ring.tile([P, BANK], U32, name="words", bufs=4, align_bytes=64)
+            nc.vector.quantize_mx(out=words[:].bitcast(FP8X4), scales=plane_s[b][:, cols], in_=woven[:])
+            nc.sync.dma_start(out=words_out[b][:, cols], in_=words[:].bitcast(I32))
+
+        def store_plane_scales(b):
+            for q in range(4):
+                nc.sync.dma_start(
+                    out=out_3[b, 4 * q : 4 * q + 4, :].bitcast(I32),
+                    in_=plane_s[b][32 * q : 32 * q + 4, :].bitcast(I32),
+                )
+
+        def quantize_x(b, woven):
+            nc.vector.quantize_mx(out=x_c[:, b, :].bitcast(FP8X4), scales=x_s[:, b, :], in_=woven[:])
+
+        w4_w = keep.tile([P, GROUPS, 2 * N], U8, name="w4_w", align_bytes=64)
+        w5_c = keep.tile([P, GROUPS, N], U32, name="w5_c", align_bytes=64)
+        w5_s = keep.tile([P, GROUPS, N], U8, name="w5_s", align_bytes=64)
+
+        def load_w4():
+            nc.sync.dma_start(out=w4_w[:].bitcast(I32), in_=w4_words.rearrange("b p n -> p b n").bitcast(I32))
+            for q in range(4):
+                nc.sync.dma_start(
+                    out=w4_s[32 * q : 32 * q + 4, :].rearrange("r (b n) -> r b n", b=GROUPS).bitcast(I32),
+                    in_=w4_scales[:, 4 * q : 4 * q + 4, :].rearrange("b r n -> r b n").bitcast(I32),
+                )
+
+        def load_w5(b):
+            raw = shared.tile([P, PACK, N], F32, name=f"raw5{b}", offset=RAW_OFFSETS[0][b])
+            nc.sync.dma_start(out=raw[:], in_=w5[b * KP : (b + 1) * KP, :].rearrange("(p j) n -> p j n", j=PACK))
+            return raw
+
+        def prepare_w5(b, raw):
+            grouped = shared.tile([P, PACK * N], BF16, name=f"grouped5{b}", align_bytes=64, offset=SLOT[b])
+            weave(nc.scalar.copy, grouped, raw[:], 0, PACK)
+            nc.vector.quantize_mx(out=w5_c[:, b, :].bitcast(FP8X4), scales=w5_s[:, b, :], in_=grouped[:])
+
+        def second_pass(b, n, y1, y2):
+            cols = slice(n * P, (n + 1) * P)
+            nc.tensor.matmul_mx(
+                out=y2[:], lhsT=w5_c[:, b, cols].bitcast(FP8X4), lhsT_scale=w5_s[:, b, cols],
+                rhs=x_c[:, b, :].bitcast(FP8X4), rhs_scale=x_s[:, b, :], start=(b == 0), stop=(b == GROUPS - 1),
+            )
+            nc.tensor.matmul_mx(
+                out=y1[:], lhsT=w4_w[:, b, 2 * n * P : 2 * (n + 1) * P].bitcast(FP4X4),
+                lhsT_scale=w4_s[:, b * N + n * P : b * N + (n + 1) * P],
+                rhs=x_c[:, b, :].bitcast(FP8X4), rhs_scale=x_s[:, b, :], start=(b == 0), stop=(b == GROUPS - 1),
+            )
+
+        tiles = GROUPS * PACK
+        pages.append(load_page(1))
+        raw1 = [load_w1(1, 0), load_w1(1, 1)]
+        pages.append(load_page(2))
+        raw1.append(load_w1(1, 2))
+        pages.append(load_page(3))
+        raw5 = [load_w5(b) for b in range(GROUPS)]
+        pages.append(load_page(4))
+        pages.append(load_page(5))
+        load_w4()
+
+        def planes0(c):
+            woven = new_woven(0, c)
+            weave(nc.scalar.copy, woven, rows0[c // 2][:, :, (c % 2) * BANK : (c % 2 + 1) * BANK], 0, PACK)
+            quantize_planes(0, c, woven)
+
+        def weave_lo(c):
+            woven1.append(new_woven(1, c))
+            weave(nc.scalar.copy, woven1[c], rows1_lo[c // 2][:, :, (c % 2) * BANK : (c % 2 + 1) * BANK], 0, 2)
+
+        ready = [features(0), features(1)]
+        woven1 = []
+        for i in range(tiles):
+            scatter(i, *ready[i])
+            fetch(i)
+            hand_out(i)
+            if i + PAGE_BUFS < tiles:
+                pages.append(load_page(i + PAGE_BUFS))
+            if i == 4:
+                planes0(0)
+                planes0(1)
+            if i == 5:
+                planes0(2)
+                planes0(3)
+                store_plane_scales(0)
+            if i + 2 < tiles:
+                ready.append(features(i + 2))
+            if i == 0:
+                for a in range(PASSES_K):
+                    prepare_w1(1, a, raw1[a])
+            if i == 2:
+                for b in range(GROUPS):
+                    prepare_w5(b, raw5[b])
+            if i == 3:
+                for t in range(PACK):
+                    add_bias(0, t, x_rows[0][:, t, :])
+                x0 = shared.tile([P, PACK * M], BF16, name="x0", align_bytes=64, offset=SLOT[2])
+                weave(nc.scalar.copy, x0, x_rows[0][:], 0, PACK)
+                quantize_x(0, x0)
+            if i == 5:
+                for c in range(CHUNKS - 1):
+                    weave_lo(c)
+            if i == 6:
+                for t in range(PACK - 1):
+                    add_bias(1, t, x_rows[1][:, t, :])
+                weave_lo(CHUNKS - 1)
+                x1 = shared.tile([P, PACK * M], BF16, name="x1", align_bytes=64, offset=SLOT[0])
+                weave(nc.scalar.copy, x1, x_rows[1][:, 0:3, :], 0, 3)
+                y = []
+                for n in range(N // P):
+                    y1 = psum.tile([P, M], F32, name="work" if n == 2 else "sums")
+                    y2 = psum.tile([P, M], F32, name="work" if n == 2 else "sums")
+                    y.append((y1, y2))
+                    second_pass(0, n, y1, y2)
+
+        last = pages[tiles - 1]
+        nc.scalar.copy(out=rows1_hi[:, 1, 0 : T2 // 2], in_=last[:, 0 : T2 // 2])
+        add_bias(1, PACK - 1, x1[:].rearrange("p (m t) -> p t m", t=PACK)[:, PACK - 1, :])
+        nc.vector.tensor_copy(out=rows1_hi[:, 1, T2 // 2 :], in_=last[:, T2 // 2 :])
+        weave(nc.vector.tensor_copy, woven1[0], rows1_hi[:, :, 0:BANK], 2, 2)
+        quantize_x(1, x1)
+        weave(nc.scalar.copy, woven1[3], rows1_hi[:, :, 3 * BANK :], 2, 2)
+        for n in range(N // P):
+            second_pass(1, n, *y[n])
+        for c in range(1, 3):
+            weave(nc.vector.tensor_copy, woven1[c], rows1_hi[:, :, c * BANK : (c + 1) * BANK], 2, 2)
+        for c in range(CHUNKS):
+            quantize_planes(1, c, woven1[c])
+        store_plane_scales(1)
+        for n in range(N // P):
+            y1, y2 = y[n]
+            phase = shared.tile([P, M], F32, name=f"phase{n}", offset=REGION_A + (24 + 2 * n) * KB)
+            nc.scalar.activation(out=phase[:], in_=y2[:], func=ACT.Tanh)
+            nc.scalar.activation(out=phase[:], in_=phase[:], func=ACT.Sin, bias=half_pi[:])
+            nc.scalar.activation(out=phase[:], in_=phase[:], func=ACT.Square, scale=math.sqrt(2.0))
+            nc.vector.scalar_tensor_tensor(out=phase[:], in0=phase[:], scalar=-1.0, in1=y1[:], op0=ALU.add, op1=ALU.mult)
+            nc.sync.dma_start(out=out_0[n * P : (n + 1) * P, :], in_=phase[:])

@@ -30,12 +30,22 @@ KB = 1024
 REGION_A, REGION_B, REGION_C, REGION_D, REGION_E = 0, 32 * KB, 56 * KB, 80 * KB, 104 * KB
 RAW_OFFSETS = [[REGION_B + 8 * KB * a for a in range(PASSES_K)], [REGION_C + 8 * KB * a for a in range(PASSES_K)]]
 SLOT = [REGION_D + 4 * KB * k for k in range(6)]
-GOT_S, GOT_W = REGION_E, [REGION_E + 9 * KB, REGION_E + KB, REGION_E + 5 * KB]
-GROUPED_OFFSETS = [[GOT_S, SLOT[5], GOT_W[2]], [SLOT[0], SLOT[1], SLOT[2]]]
-ACT_OFFSETS = [SLOT[1], SLOT[3], SLOT[5], SLOT[3], SLOT[5], SLOT[3], SLOT[5], SLOT[3]]
-FACTOR_OFFSETS = [SLOT[0], SLOT[2], SLOT[4], RAW_OFFSETS[1][2], SLOT[4], RAW_OFFSETS[0][1], REGION_A, REGION_A + 16 * KB]
-WOVEN_OFFSETS = [[REGION_C + 4 * KB * c for c in range(CHUNKS)], [REGION_C + 4 * KB * ((c + 4) % 6) for c in range(CHUNKS)]]
+GOT_S, GOT_W = REGION_E + 4 * KB, [REGION_E + 5 * KB, REGION_E, REGION_E + 9 * KB]
+WGS_OFFSET = REGION_E + 2 * KB
+REGION_F = REGION_E + 13 * KB
+RAW10, RAW11, RAW12 = RAW_OFFSETS[1]
+GROUPED_OFFSETS = [[SLOT[4], SLOT[5], GOT_W[2]], [REGION_F, RAW10, RAW11 + 2 * KB]]
+GROUPED5_OFFSETS = [RAW11, RAW11 + 3 * KB]
+ACT_OFFSETS = [SLOT[2], SLOT[3], SLOT[5], RAW12 + 4 * KB, SLOT[2], RAW_OFFSETS[0][0], SLOT[4], SLOT[3]]
+FACTOR_OFFSETS = [SLOT[0], SLOT[1], SLOT[4], RAW12, SLOT[0], RAW_OFFSETS[0][1], REGION_A, REGION_A + 16 * KB]
+X_ROWS_OFFSETS = [RAW10 + 2 * KB, RAW12]
+ROWS1_LO_OFFSETS = [RAW12, RAW_OFFSETS[0][2]]
+GAIN_OFFSETS = {2: REGION_F, 5: X_ROWS_OFFSETS[0]}
+WOVEN_OFFSETS = [RAW10 + 4 * KB * c for c in range(CHUNKS)]
 HALF = T2 // 2
+FACTOR_BANKS = [(2, 3), (4, 5), (2, 1), (4, 5)] + [(2, 3), (4, 5)] * 2
+ACT_BANKS = [(6, 7), (0, 1), (3, 1), (6, 7)] + [(0, 1), (6, 7)] * 2
+SUM_BANKS = [(4, 5), (6, 7), (2, 3)]
 
 
 def tile_list_cue_brightness_desk_kernel(
@@ -48,7 +58,7 @@ def tile_list_cue_brightness_desk_kernel(
         keep = ctx.enter_context(tc.tile_pool(name="keep", bufs=1))
         shared = ctx.enter_context(tc.tile_pool(name="shared", bufs=1))
         ring = ctx.enter_context(tc.tile_pool(name="ring", bufs=2))
-        psum = ctx.enter_context(tc.psum_pool(name="psum", bufs=4))
+        psum = ctx.enter_context(tc.psum_pool(name="psum", bufs=1))
 
         page_in = page0.rearrange("(b p t) m -> b t p m", b=GROUPS, t=PACK)
         page_out = out_1.rearrange("(b p t) m -> b t p m", b=GROUPS, t=PACK)
@@ -69,7 +79,7 @@ def tile_list_cue_brightness_desk_kernel(
         nc.vector.tensor_scalar(half_pi[:], one[:], math.pi / 2, None, ALU.mult)
 
         for q in range(4):
-            nc.scalar.dma_start(
+            nc.gpsimd.dma_start(
                 out=tab_s[32 * q : 32 * q + 4 * PASSES_K, :].bitcast(I32),
                 in_=tab_scales[:, 4 * q : 4 * q + 4, :].bitcast(I32),
             )
@@ -82,6 +92,9 @@ def tile_list_cue_brightness_desk_kernel(
         w1_c = keep.tile([P, GROUPS * PASSES_K, KP], U32, name="w1_c", align_bytes=64)
         w1_s = keep.tile([P, GROUPS * PASSES_K, KP], U8, name="w1_s", align_bytes=64)
         wgs_t = keep.tile([P, S // P * PACK * P], F32, name="wgs_t")
+
+        def new_bank(name, number):
+            return psum.tile([P, BANK], F32, name=name, offset=number * BANK * 4)
 
         def load_table(a):
             nc.sync.dma_start(out=tab_w[a][:], in_=tab_words[a].rearrange("p t i -> p (t i)").bitcast(I32))
@@ -113,13 +126,13 @@ def tile_list_cue_brightness_desk_kernel(
             return page
 
         nc.sync.dma_start(idx1[:], offs)
-        wgs_sb = shared.tile([P, S], F32, name="wgs_sb", offset=SLOT[4])
+        wgs_sb = shared.tile([P, S], F32, name="wgs_sb", offset=WGS_OFFSET)
         nc.sync.dma_start(out=wgs_sb[:], in_=wgs)
         load_table(0)
         nc.sync.dma_start(out=gain_c[:], in_=gain.rearrange("(b p t) -> p b t", b=GROUPS, t=PACK))
         raw00 = load_w1(0, 0)
-        load_table(1)
         raw01 = load_w1(0, 1)
+        load_table(1)
         raw02 = load_w1(0, 2)
         load_table(2)
         nc.sync.dma_start(idx2[:], offs2)
@@ -129,53 +142,69 @@ def tile_list_cue_brightness_desk_kernel(
 
         dealt = wgs_t[:].rearrange("j (jb t r q) -> j jb t r q", t=PACK, r=4, q=32)
         for half in range(2):
-            bank = psum.tile([P, BANK], F32, name="work")
+            bank = new_bank(f"turned{half}", half)
             for jj in range(4):
                 jb = 4 * half + jj
                 nc.tensor.transpose(bank[:, jj * P : (jj + 1) * P], wgs_sb[:, jb * P : (jb + 1) * P], ident[:])
-            nc.scalar.copy(
+            nc.vector.tensor_copy(
                 out=dealt[:, 4 * half : 4 * half + 4, :, 0, :],
                 in_=bank[:].rearrange("j (jb q t) -> j jb t q", q=32, t=PACK),
             )
-        gather_table(0, 0)
-        gather_table(0, 1)
         for r in range(1, 4):
             nc.vector.tensor_copy(out=dealt[:, :, :, r, :], in_=dealt[:, :, :, 0, :])
+        gather_table(0, 0)
+        gather_table(0, 1)
+        nc.vector.tensor_copy(got_s[:], tab_s[:].indirect(idx1[:]))
         prepare_w1(0, 0, raw00)
         gather_table(1, 0)
         gather_table(1, 1)
-        nc.vector.tensor_copy(got_s[:], tab_s[:].indirect(idx1[:]))
         prepare_w1(0, 1, raw01)
         prepare_w1(0, 2, raw02)
         gather_table(2, 0)
         gather_table(2, 1)
 
-        def features(i):
-            b, t = divmod(i, PACK)
+        gain_of = [gain_c[:, i // PACK, i % PACK : i % PACK + 1] for i in range(GROUPS * PACK)]
+
+        def make_factor(i):
+            t = i % PACK
+            if i in GAIN_OFFSETS:
+                gain_i = shared.tile([P, 1], F32, name=f"gain{i}", offset=GAIN_OFFSETS[i])
+                nc.gpsimd.tensor_copy(gain_i[:], gain_of[i])
+                gain_of[i] = gain_i[:]
             factor = shared.tile([P, S], F32, name=f"factor{i}", offset=FACTOR_OFFSETS[i])
-            act = shared.tile([P, S], F32, name=f"act{i}", offset=ACT_OFFSETS[i])
             for half in range(2):
                 cols = slice(half * BANK, (half + 1) * BANK)
-                bank = psum.tile([P, BANK], F32, name="work")
+                bank = new_bank(f"factor_bank{i}{half}", FACTOR_BANKS[i][half])
                 for jj in range(4):
                     start = ((4 * half + jj) * PACK + t) * P
                     nc.tensor.transpose(bank[:, jj * P : (jj + 1) * P], wgs_t[:, start : start + P], ident[:])
-                nc.scalar.activation(out=factor[:, cols], in_=bank[:], func=ACT.Copy, scale=gain_c[:, b, t : t + 1])
+                nc.scalar.activation(out=factor[:, cols], in_=bank[:], func=ACT.Copy, scale=gain_of[i])
+            return factor
+
+        def new_act(i):
+            return shared.tile([P, S], F32, name=f"act{i}", offset=ACT_OFFSETS[i])
+
+        def make_act(i, act, half):
+            b, t = divmod(i, PACK)
+            cols = slice(half * BANK, (half + 1) * BANK)
+            acc = new_bank(f"act_bank{i}{half}", ACT_BANKS[i][half])
+            for a in range(PASSES_K):
+                g = b * PASSES_K + a
+                nc.tensor.matmul_mx(
+                    out=acc[:],
+                    lhsT=w1_c[:, g, t * P : (t + 1) * P].bitcast(FP8X4),
+                    lhsT_scale=w1_s[:, g, t * P : (t + 1) * P],
+                    rhs=got_w[a][:, cols].bitcast(FP8X4),
+                    rhs_scale=got_s[4 * a : P, cols],
+                    start=(a == 0),
+                    stop=(a == PASSES_K - 1),
+                )
+            nc.scalar.activation(out=act[:, cols], in_=acc[:], func=ACT.Silu)
+
+        def features(i):
+            factor, act = make_factor(i), new_act(i)
             for half in range(2):
-                cols = slice(half * BANK, (half + 1) * BANK)
-                acc = psum.tile([P, BANK], F32, name="work")
-                for a in range(PASSES_K):
-                    g = b * PASSES_K + a
-                    nc.tensor.matmul_mx(
-                        out=acc[:],
-                        lhsT=w1_c[:, g, t * P : (t + 1) * P].bitcast(FP8X4),
-                        lhsT_scale=w1_s[:, g, t * P : (t + 1) * P],
-                        rhs=got_w[a][:, cols].bitcast(FP8X4),
-                        rhs_scale=got_s[4 * a : P, cols],
-                        start=(a == 0),
-                        stop=(a == PASSES_K - 1),
-                    )
-                nc.scalar.activation(out=act[:, cols], in_=acc[:], func=ACT.Silu)
+                make_act(i, act, half)
             return act, factor
 
         def scatter(i, act, factor):
@@ -190,9 +219,9 @@ def tile_list_cue_brightness_desk_kernel(
                 )
 
         rows0 = [shared.tile([P, PACK, HALF], F32, name=f"rows0{h}", offset=REGION_A + 16 * KB * h) for h in range(2)]
-        rows1_lo = [shared.tile([P, 2, HALF], F32, name=f"rows1_lo{h}", offset=REGION_B + 16 * KB * h) for h in range(2)]
+        rows1_lo = [shared.tile([P, 2, HALF], F32, name=f"rows1_lo{h}", offset=ROWS1_LO_OFFSETS[h]) for h in range(2)]
         rows1_hi = shared.tile([P, 2, T2], F32, name="rows1_hi", offset=REGION_A)
-        x_rows = [shared.tile([P, PACK, M], BF16, name=f"x_rows{b}", offset=REGION_B) for b in range(GROUPS)]
+        x_rows = [shared.tile([P, PACK, M], BF16, name=f"x_rows{b}", offset=X_ROWS_OFFSETS[b]) for b in range(GROUPS)]
         x_c = keep.tile([P, GROUPS, M], U32, name="x_c", align_bytes=64)
         x_s = keep.tile([P, GROUPS, M], U8, name="x_s", align_bytes=64)
         plane_s = [keep.tile([P, T2], U8, name=f"plane_s{b}", align_bytes=64) for b in range(GROUPS)]
@@ -225,7 +254,7 @@ def tile_list_cue_brightness_desk_kernel(
 
         def new_woven(b, c):
             return shared.tile(
-                [P, PACK * BANK], BF16, name=f"woven{b}{c}", align_bytes=64, offset=WOVEN_OFFSETS[b][c]
+                [P, PACK * BANK], BF16, name=f"woven{b}{c}", align_bytes=64, offset=WOVEN_OFFSETS[c]
             )
 
         def quantize_planes(b, c, woven):
@@ -262,7 +291,7 @@ def tile_list_cue_brightness_desk_kernel(
             return raw
 
         def prepare_w5(b, raw):
-            grouped = shared.tile([P, PACK * N], BF16, name=f"grouped5{b}", align_bytes=64, offset=SLOT[b])
+            grouped = shared.tile([P, PACK * N], BF16, name=f"grouped5{b}", align_bytes=64, offset=GROUPED5_OFFSETS[b])
             weave(nc.scalar.copy, grouped, raw[:], 0, PACK)
             nc.vector.quantize_mx(out=w5_c[:, b, :].bitcast(FP8X4), scales=w5_s[:, b, :], in_=grouped[:])
 
@@ -298,7 +327,13 @@ def tile_list_cue_brightness_desk_kernel(
             woven1.append(new_woven(1, c))
             weave(nc.scalar.copy, woven1[c], rows1_lo[c // 2][:, :, (c % 2) * BANK : (c % 2 + 1) * BANK], 0, 2)
 
-        ready = [features(0), features(1)]
+        factor0, factor1, act0, act1 = make_factor(0), make_factor(1), new_act(0), new_act(1)
+        for i, act, half in ((0, act0, 0), (0, act0, 1), (1, act1, 0), (1, act1, 1)):
+            make_act(i, act, half)
+        act2 = new_act(2)
+        for half in range(2):
+            make_act(2, act2, half)
+        ready = [(act0, factor0), (act1, factor1), (act2, make_factor(2))]
         woven1 = []
         for i in range(tiles):
             scatter(i, *ready[i])
@@ -313,18 +348,18 @@ def tile_list_cue_brightness_desk_kernel(
                 planes0(2)
                 planes0(3)
                 store_plane_scales(0)
-            if i + 2 < tiles:
+            if i == 2:
+                for b in range(GROUPS):
+                    prepare_w5(b, raw5[b])
+            if 0 < i < tiles - 2:
                 ready.append(features(i + 2))
             if i == 0:
                 for a in range(PASSES_K):
                     prepare_w1(1, a, raw1[a])
-            if i == 2:
-                for b in range(GROUPS):
-                    prepare_w5(b, raw5[b])
             if i == 3:
                 for t in range(PACK):
                     add_bias(0, t, x_rows[0][:, t, :])
-                x0 = shared.tile([P, PACK * M], BF16, name="x0", align_bytes=64, offset=SLOT[2])
+                x0 = shared.tile([P, PACK * M], BF16, name="x0", align_bytes=64, offset=SLOT[1])
                 weave(nc.scalar.copy, x0, x_rows[0][:], 0, PACK)
                 quantize_x(0, x0)
             if i == 5:
@@ -334,12 +369,12 @@ def tile_list_cue_brightness_desk_kernel(
                 for t in range(PACK - 1):
                     add_bias(1, t, x_rows[1][:, t, :])
                 weave_lo(CHUNKS - 1)
-                x1 = shared.tile([P, PACK * M], BF16, name="x1", align_bytes=64, offset=SLOT[0])
+                x1 = shared.tile([P, PACK * M], BF16, name="x1", align_bytes=64, offset=SLOT[5])
                 weave(nc.scalar.copy, x1, x_rows[1][:, 0:3, :], 0, 3)
                 y = []
                 for n in range(N // P):
-                    y1 = psum.tile([P, M], F32, name="work" if n == 2 else "sums")
-                    y2 = psum.tile([P, M], F32, name="work" if n == 2 else "sums")
+                    y1 = new_bank(f"y1_{n}", SUM_BANKS[n][0])
+                    y2 = new_bank(f"y2_{n}", SUM_BANKS[n][1])
                     y.append((y1, y2))
                     second_pass(0, n, y1, y2)
 

import math
from contextlib import ExitStack

import concourse.mybir as mybir
from concourse.masks import make_identity

K, T, S, H, T2, M, N = 1536, 2048, 1024, 1024, 2048, 512, 384
FLOPS = 2 * K * H * S + 2 * 2 * H * N * M

F32 = mybir.dt.float32
BF16 = mybir.dt.bfloat16
I32 = mybir.dt.int32
U32 = mybir.dt.uint32
U16 = mybir.dt.uint16
U8 = mybir.dt.uint8
FP8X4 = mybir.dt.float8_e4m3fn_x4
FP4X4 = mybir.dt.float4_e2m1fn_x4
ACT = mybir.ActivationFunctionType
ALU = mybir.AluOpType

P = 128
PACK = 4
KP = P * PACK
BANK = 512
PASSES_K = K // KP
GROUPS = H // KP
CHUNKS = T2 // BANK
PAGE_BUFS = 6
KB = 1024
REGION_A, REGION_B, REGION_C, REGION_D, REGION_E = 0, 32 * KB, 56 * KB, 80 * KB, 104 * KB
RAW_OFFSETS = [[REGION_B + 8 * KB * a for a in range(PASSES_K)], [REGION_C + 8 * KB * a for a in range(PASSES_K)]]
SLOT = [REGION_D + 4 * KB * k for k in range(6)]
GOT_S, GOT_W = REGION_E + 4 * KB, [REGION_E + 5 * KB, REGION_E, REGION_E + 9 * KB]
WGS_OFFSET = REGION_E + 2 * KB
REGION_F = REGION_E + 13 * KB
RAW10, RAW11, RAW12 = RAW_OFFSETS[1]
GROUPED_OFFSETS = [[SLOT[4], SLOT[5], GOT_W[2]], [REGION_F, RAW10, RAW11 + 2 * KB]]
GROUPED5_OFFSETS = [RAW11, RAW11 + 3 * KB]
ACT_OFFSETS = [SLOT[2], SLOT[3], SLOT[5], RAW12 + 4 * KB, SLOT[2], RAW_OFFSETS[0][0], SLOT[4], SLOT[3]]
FACTOR_OFFSETS = [SLOT[0], SLOT[1], SLOT[4], RAW12, SLOT[0], RAW_OFFSETS[0][1], REGION_A, REGION_A + 16 * KB]
X_ROWS_OFFSETS = [RAW10 + 2 * KB, RAW12]
ROWS1_LO_OFFSETS = [RAW12, RAW_OFFSETS[0][2]]
GAIN_OFFSETS = {2: REGION_F, 5: X_ROWS_OFFSETS[0]}
WOVEN_OFFSETS = [RAW10 + 4 * KB * c for c in range(CHUNKS)]
HALF = T2 // 2
FACTOR_BANKS = [(2, 3), (4, 5), (2, 1), (4, 5)] + [(2, 3), (4, 5)] * 2
ACT_BANKS = [(6, 7), (0, 1), (3, 1), (6, 7)] + [(0, 1), (6, 7)] * 2
SUM_BANKS = [(4, 5), (6, 7), (2, 3)]


def tile_list_cue_brightness_desk_kernel(
    tc, tab_words, tab_scales, offs, offs2, offs3, w1, gain, wgs, page0, bx, w4_words, w4_scales, w5,
    out_0, out_1, out_2, out_3,
):
    nc = tc.nc
    with ExitStack() as ctx:
        lists = ctx.enter_context(tc.tile_pool(name="lists", bufs=1))
        keep = ctx.enter_context(tc.tile_pool(name="keep", bufs=1))
        shared = ctx.enter_context(tc.tile_pool(name="shared", bufs=1))
        ring = ctx.enter_context(tc.tile_pool(name="ring", bufs=2))
        psum = ctx.enter_context(tc.psum_pool(name="psum", bufs=1))

        page_in = page0.rearrange("(b p t) m -> b t p m", b=GROUPS, t=PACK)
        page_out = out_1.rearrange("(b p t) m -> b t p m", b=GROUPS, t=PACK)

        idx1 = lists.tile([P, S // 16], U16, name="idx1")
        idx2 = lists.tile([P, S // 16], U16, name="idx2")
        idx3 = lists.tile([P, M // 16], U16, name="idx3")

        ident = keep.tile([P, P], F32, name="ident")
        make_identity(nc, ident[:])
        tab_s = keep.tile([P, T], U8, name="tab_s", align_bytes=64)
        nc.vector.memset(tab_s[:].bitcast(I32), 0)
        w4_s = keep.tile([P, GROUPS * N], U8, name="w4_s", align_bytes=64)
        nc.vector.memset(w4_s[:].bitcast(I32), 0)
        half_pi = keep.tile([P, 1], F32, name="half_pi")
        one = keep.tile([P, 1], F32, name="one")
        nc.vector.memset(one[:], 1.0)
        nc.vector.tensor_scalar(half_pi[:], one[:], math.pi / 2, None, ALU.mult)

        for q in range(4):
            nc.gpsimd.dma_start(
                out=tab_s[32 * q : 32 * q + 4 * PASSES_K, :].bitcast(I32),
                in_=tab_scales[:, 4 * q : 4 * q + 4, :].bitcast(I32),
            )
        gain_c = keep.tile([P, GROUPS, PACK], F32, name="gain_c")
        bx_c = keep.tile([P, GROUPS, PACK], F32, name="bx_c")

        tab_w = [shared.tile([P, T], I32, name=f"tab_w{a}", offset=a * T * 4) for a in range(PASSES_K)]
        got_w = [shared.tile([P, S], U32, name=f"got_w{a}", align_bytes=64, offset=GOT_W[a]) for a in range(PASSES_K)]
        got_s = shared.tile([P, S], U8, name="got_s", align_bytes=64, offset=GOT_S)
        w1_c = keep.tile([P, GROUPS * PASSES_K, KP], U32, name="w1_c", align_bytes=64)
        w1_s = keep.tile([P, GROUPS * PASSES_K, KP], U8, name="w1_s", align_bytes=64)
        wgs_t = keep.tile([P, S // P * PACK * P], F32, name="wgs_t")

        def new_bank(name, number):
            return psum.tile([P, BANK], F32, name=name, offset=number * BANK * 4)

        def load_table(a):
            nc.sync.dma_start(out=tab_w[a][:], in_=tab_words[a].rearrange("p t i -> p (t i)").bitcast(I32))

        def gather_table(a, half):
            cols = slice(half * BANK, (half + 1) * BANK)
            nc.vector.tensor_copy(got_w[a][:, cols], tab_w[a][:].bitcast(U32).indirect(idx1[:, half * 32 : (half + 1) * 32]))

        def load_w1(b, a):
            raw = shared.tile([P, PACK, KP], F32, name=f"raw{b}{a}", offset=RAW_OFFSETS[b][a])
            rows = w1[a * KP : (a + 1) * KP, b * KP : (b + 1) * KP]
            nc.sync.dma_start(out=raw[:], in_=rows.rearrange("(p j) c -> p j c", j=PACK))
            return raw

        def prepare_w1(b, a, raw):
            grouped = shared.tile(
                [P, PACK * KP], BF16, name=f"grouped{b}{a}", align_bytes=64, offset=GROUPED_OFFSETS[b][a]
            )
            nc.scalar.copy(
                out=grouped[:].rearrange("p (t m j) -> p m j t", t=PACK, j=PACK),
                in_=raw[:].rearrange("p j (m t) -> p m j t", t=PACK),
            )
            g = b * PASSES_K + a
            nc.vector.quantize_mx(out=w1_c[:, g, :].bitcast(FP8X4), scales=w1_s[:, g, :], in_=grouped[:])

        def load_page(i):
            page = ring.tile([P, T2], F32, name="page", bufs=PAGE_BUFS)
            nc.sync.dma_start(out=page[:], in_=page_in[i // PACK, i % PACK])
            return page

        nc.sync.dma_start(idx1[:], offs)
        wgs_sb = shared.tile([P, S], F32, name="wgs_sb", offset=WGS_OFFSET)
        nc.sync.dma_start(out=wgs_sb[:], in_=wgs)
        load_table(0)
        nc.sync.dma_start(out=gain_c[:], in_=gain.rearrange("(b p t) -> p b t", b=GROUPS, t=PACK))
        raw00 = load_w1(0, 0)
        raw01 = load_w1(0, 1)
        load_table(1)
        raw02 = load_w1(0, 2)
        load_table(2)
        nc.sync.dma_start(idx2[:], offs2)
        pages = [load_page(0)]
        nc.sync.dma_start(idx3[:], offs3)
        nc.sync.dma_start(out=bx_c[:], in_=bx.rearrange("(b p t) -> p b t", b=GROUPS, t=PACK))

        dealt = wgs_t[:].rearrange("j (jb t r q) -> j jb t r q", t=PACK, r=4, q=32)
        for half in range(2):
            bank = new_bank(f"turned{half}", half)
            for jj in range(4):
                jb = 4 * half + jj
                nc.tensor.transpose(bank[:, jj * P : (jj + 1) * P], wgs_sb[:, jb * P : (jb + 1) * P], ident[:])
            nc.vector.tensor_copy(
                out=dealt[:, 4 * half : 4 * half + 4, :, 0, :],
                in_=bank[:].rearrange("j (jb q t) -> j jb t q", q=32, t=PACK),
            )
        for r in range(1, 4):
            nc.vector.tensor_copy(out=dealt[:, :, :, r, :], in_=dealt[:, :, :, 0, :])
        gather_table(0, 0)
        gather_table(0, 1)
        nc.vector.tensor_copy(got_s[:], tab_s[:].indirect(idx1[:]))
        prepare_w1(0, 0, raw00)
        gather_table(1, 0)
        gather_table(1, 1)
        prepare_w1(0, 1, raw01)
        prepare_w1(0, 2, raw02)
        gather_table(2, 0)
        gather_table(2, 1)

        gain_of = [gain_c[:, i // PACK, i % PACK : i % PACK + 1] for i in range(GROUPS * PACK)]

        def make_factor(i):
            t = i % PACK
            if i in GAIN_OFFSETS:
                gain_i = shared.tile([P, 1], F32, name=f"gain{i}", offset=GAIN_OFFSETS[i])
                nc.gpsimd.tensor_copy(gain_i[:], gain_of[i])
                gain_of[i] = gain_i[:]
            factor = shared.tile([P, S], F32, name=f"factor{i}", offset=FACTOR_OFFSETS[i])
            for half in range(2):
                cols = slice(half * BANK, (half + 1) * BANK)
                bank = new_bank(f"factor_bank{i}{half}", FACTOR_BANKS[i][half])
                for jj in range(4):
                    start = ((4 * half + jj) * PACK + t) * P
                    nc.tensor.transpose(bank[:, jj * P : (jj + 1) * P], wgs_t[:, start : start + P], ident[:])
                nc.scalar.activation(out=factor[:, cols], in_=bank[:], func=ACT.Copy, scale=gain_of[i])
            return factor

        def new_act(i):
            return shared.tile([P, S], F32, name=f"act{i}", offset=ACT_OFFSETS[i])

        def make_act(i, act, half):
            b, t = divmod(i, PACK)
            cols = slice(half * BANK, (half + 1) * BANK)
            acc = new_bank(f"act_bank{i}{half}", ACT_BANKS[i][half])
            for a in range(PASSES_K):
                g = b * PASSES_K + a
                nc.tensor.matmul_mx(
                    out=acc[:],
                    lhsT=w1_c[:, g, t * P : (t + 1) * P].bitcast(FP8X4),
                    lhsT_scale=w1_s[:, g, t * P : (t + 1) * P],
                    rhs=got_w[a][:, cols].bitcast(FP8X4),
                    rhs_scale=got_s[4 * a : P, cols],
                    start=(a == 0),
                    stop=(a == PASSES_K - 1),
                )
            nc.scalar.activation(out=act[:, cols], in_=acc[:], func=ACT.Silu)

        def features(i):
            factor, act = make_factor(i), new_act(i)
            for half in range(2):
                make_act(i, act, half)
            return act, factor

        def scatter(i, act, factor):
            pieces = 2 if i == 0 else 1
            n = S // pieces
            for k in range(pieces):
                nc.vector.tensor_tensor(
                    pages[i][:].indirect(idx2[:, k * n // 16 : (k + 1) * n // 16]),
                    act[:, k * n : (k + 1) * n],
                    factor[:, k * n : (k + 1) * n],
                    ALU.mult,
                )

        rows0 = [shared.tile([P, PACK, HALF], F32, name=f"rows0{h}", offset=REGION_A + 16 * KB * h) for h in range(2)]
        rows1_lo = [shared.tile([P, 2, HALF], F32, name=f"rows1_lo{h}", offset=ROWS1_LO_OFFSETS[h]) for h in range(2)]
        rows1_hi = shared.tile([P, 2, T2], F32, name="rows1_hi", offset=REGION_A)
        x_rows = [shared.tile([P, PACK, M], BF16, name=f"x_rows{b}", offset=X_ROWS_OFFSETS[b]) for b in range(GROUPS)]
        x_c = keep.tile([P, GROUPS, M], U32, name="x_c", align_bytes=64)
        x_s = keep.tile([P, GROUPS, M], U8, name="x_s", align_bytes=64)
        plane_s = [keep.tile([P, T2], U8, name=f"plane_s{b}", align_bytes=64) for b in range(GROUPS)]
        words_out = [out_2[b].rearrange("p m i -> p (m i)").bitcast(I32) for b in range(GROUPS)]

        picked = [ring.tile([P, PACK, M], F32, name="picked", bufs=1) for b in range(GROUPS)]

        def fetch(i):
            b, t = divmod(i, PACK)
            nc.vector.tensor_copy(picked[b][:, t, :], pages[i][:].indirect(idx3[:]))

        def hand_out(i):
            b, t = divmod(i, PACK)
            if i < PACK + 2:
                for h in range(2):
                    rows = rows0[h] if b == 0 else rows1_lo[h]
                    nc.sync.dma_start(out=rows[:, t, :], in_=pages[i][:, h * HALF : (h + 1) * HALF])
            elif i == PACK + 2:
                nc.sync.dma_start(out=rows1_hi[:, 0, :], in_=pages[i][:])
            nc.sync.dma_start(out=page_out[b, t], in_=pages[i][:])

        def add_bias(b, t, out):
            nc.scalar.activation(out=out, in_=picked[b][:, t, :], func=ACT.Identity, bias=bx_c[:, b, t : t + 1])

        def weave(copy, woven, rows, first, count):
            copy(
                out=woven[:].rearrange("p (c i t) -> p c t i", i=4, t=PACK)[:, :, first : first + count, :],
                in_=rows.rearrange("p t (c i) -> p c t i", i=4),
            )

        def new_woven(b, c):
            return shared.tile(
                [P, PACK * BANK], BF16, name=f"woven{b}{c}", align_bytes=64, offset=WOVEN_OFFSETS[c]
            )

        def quantize_planes(b, c, woven):
            cols = slice(c * BANK, (c + 1) * BANK)
            words = ring.tile([P, BANK], U32, name="words", bufs=4, align_bytes=64)
            nc.vector.quantize_mx(out=words[:].bitcast(FP8X4), scales=plane_s[b][:, cols], in_=woven[:])
            nc.sync.dma_start(out=words_out[b][:, cols], in_=words[:].bitcast(I32))

        def store_plane_scales(b):
            for q in range(4):
                nc.sync.dma_start(
                    out=out_3[b, 4 * q : 4 * q + 4, :].bitcast(I32),
                    in_=plane_s[b][32 * q : 32 * q + 4, :].bitcast(I32),
                )

        def quantize_x(b, woven):
            nc.vector.quantize_mx(out=x_c[:, b, :].bitcast(FP8X4), scales=x_s[:, b, :], in_=woven[:])

        w4_w = keep.tile([P, GROUPS, 2 * N], U8, name="w4_w", align_bytes=64)
        w5_c = keep.tile([P, GROUPS, N], U32, name="w5_c", align_bytes=64)
        w5_s = keep.tile([P, GROUPS, N], U8, name="w5_s", align_bytes=64)

        def load_w4():
            nc.sync.dma_start(out=w4_w[:].bitcast(I32), in_=w4_words.rearrange("b p n -> p b n").bitcast(I32))
            for q in range(4):
                nc.sync.dma_start(
                    out=w4_s[32 * q : 32 * q + 4, :].rearrange("r (b n) -> r b n", b=GROUPS).bitcast(I32),
                    in_=w4_scales[:, 4 * q : 4 * q + 4, :].rearrange("b r n -> r b n").bitcast(I32),
                )

        def load_w5(b):
            raw = shared.tile([P, PACK, N], F32, name=f"raw5{b}", offset=RAW_OFFSETS[0][b])
            nc.sync.dma_start(out=raw[:], in_=w5[b * KP : (b + 1) * KP, :].rearrange("(p j) n -> p j n", j=PACK))
            return raw

        def prepare_w5(b, raw):
            grouped = shared.tile([P, PACK * N], BF16, name=f"grouped5{b}", align_bytes=64, offset=GROUPED5_OFFSETS[b])
            weave(nc.scalar.copy, grouped, raw[:], 0, PACK)
            nc.vector.quantize_mx(out=w5_c[:, b, :].bitcast(FP8X4), scales=w5_s[:, b, :], in_=grouped[:])

        def second_pass(b, n, y1, y2):
            cols = slice(n * P, (n + 1) * P)
            nc.tensor.matmul_mx(
                out=y2[:], lhsT=w5_c[:, b, cols].bitcast(FP8X4), lhsT_scale=w5_s[:, b, cols],
                rhs=x_c[:, b, :].bitcast(FP8X4), rhs_scale=x_s[:, b, :], start=(b == 0), stop=(b == GROUPS - 1),
            )
            nc.tensor.matmul_mx(
                out=y1[:], lhsT=w4_w[:, b, 2 * n * P : 2 * (n + 1) * P].bitcast(FP4X4),
                lhsT_scale=w4_s[:, b * N + n * P : b * N + (n + 1) * P],
                rhs=x_c[:, b, :].bitcast(FP8X4), rhs_scale=x_s[:, b, :], start=(b == 0), stop=(b == GROUPS - 1),
            )

        tiles = GROUPS * PACK
        pages.append(load_page(1))
        raw1 = [load_w1(1, 0), load_w1(1, 1)]
        pages.append(load_page(2))
        raw1.append(load_w1(1, 2))
        pages.append(load_page(3))
        raw5 = [load_w5(b) for b in range(GROUPS)]
        pages.append(load_page(4))
        pages.append(load_page(5))
        load_w4()

        def planes0(c):
            woven = new_woven(0, c)
            weave(nc.scalar.copy, woven, rows0[c // 2][:, :, (c % 2) * BANK : (c % 2 + 1) * BANK], 0, PACK)
            quantize_planes(0, c, woven)

        def weave_lo(c):
            woven1.append(new_woven(1, c))
            weave(nc.scalar.copy, woven1[c], rows1_lo[c // 2][:, :, (c % 2) * BANK : (c % 2 + 1) * BANK], 0, 2)

        factor0, factor1, act0, act1 = make_factor(0), make_factor(1), new_act(0), new_act(1)
        for i, act, half in ((0, act0, 0), (0, act0, 1), (1, act1, 0), (1, act1, 1)):
            make_act(i, act, half)
        act2 = new_act(2)
        for half in range(2):
            make_act(2, act2, half)
        ready = [(act0, factor0), (act1, factor1), (act2, make_factor(2))]
        woven1 = []
        for i in range(tiles):
            scatter(i, *ready[i])
            fetch(i)
            hand_out(i)
            if i + PAGE_BUFS < tiles:
                pages.append(load_page(i + PAGE_BUFS))
            if i == 4:
                planes0(0)
                planes0(1)
            if i == 5:
                planes0(2)
                planes0(3)
                store_plane_scales(0)
            if i == 2:
                for b in range(GROUPS):
                    prepare_w5(b, raw5[b])
            if 0 < i < tiles - 2:
                ready.append(features(i + 2))
            if i == 0:
                for a in range(PASSES_K):
                    prepare_w1(1, a, raw1[a])
            if i == 3:
                for t in range(PACK):
                    add_bias(0, t, x_rows[0][:, t, :])
                x0 = shared.tile([P, PACK * M], BF16, name="x0", align_bytes=64, offset=SLOT[1])
                weave(nc.scalar.copy, x0, x_rows[0][:], 0, PACK)
                quantize_x(0, x0)
            if i == 5:
                for c in range(CHUNKS - 1):
                    weave_lo(c)
            if i == 6:
                for t in range(PACK - 1):
                    add_bias(1, t, x_rows[1][:, t, :])
                weave_lo(CHUNKS - 1)
                x1 = shared.tile([P, PACK * M], BF16, name="x1", align_bytes=64, offset=SLOT[5])
                weave(nc.scalar.copy, x1, x_rows[1][:, 0:3, :], 0, 3)
                y = []
                for n in range(N // P):
                    y1 = new_bank(f"y1_{n}", SUM_BANKS[n][0])
                    y2 = new_bank(f"y2_{n}", SUM_BANKS[n][1])
                    y.append((y1, y2))
                    second_pass(0, n, y1, y2)

        last = pages[tiles - 1]
        nc.scalar.copy(out=rows1_hi[:, 1, 0 : T2 // 2], in_=last[:, 0 : T2 // 2])
        add_bias(1, PACK - 1, x1[:].rearrange("p (m t) -> p t m", t=PACK)[:, PACK - 1, :])
        nc.vector.tensor_copy(out=rows1_hi[:, 1, T2 // 2 :], in_=last[:, T2 // 2 :])
        weave(nc.vector.tensor_copy, woven1[0], rows1_hi[:, :, 0:BANK], 2, 2)
        quantize_x(1, x1)
        weave(nc.scalar.copy, woven1[3], rows1_hi[:, :, 3 * BANK :], 2, 2)
        for n in range(N // P):
            second_pass(1, n, *y[n])
        for c in range(1, 3):
            weave(nc.vector.tensor_copy, woven1[c], rows1_hi[:, :, c * BANK : (c + 1) * BANK], 2, 2)
        for c in range(CHUNKS):
            quantize_planes(1, c, woven1[c])
        store_plane_scales(1)
        for n in range(N // P):
            y1, y2 = y[n]
            phase = shared.tile([P, M], F32, name=f"phase{n}", offset=REGION_A + (24 + 2 * n) * KB)
            nc.scalar.activation(out=phase[:], in_=y2[:], func=ACT.Tanh)
            nc.scalar.activation(out=phase[:], in_=phase[:], func=ACT.Sin, bias=half_pi[:])
            nc.scalar.activation(out=phase[:], in_=phase[:], func=ACT.Square, scale=math.sqrt(2.0))
            nc.vector.scalar_tensor_tensor(out=phase[:], in0=phase[:], scalar=-1.0, in1=y1[:], op0=ALU.add, op1=ALU.mult)
            nc.sync.dma_start(out=out_0[n * P : (n + 1) * P, :], in_=phase[:])
